import numpy as np
import ml_dtypes


def mxq(x, axis, fmt="e4m3"):
    dtype, down = {"e4m3": (ml_dtypes.float8_e4m3fn, 7), "e5m2": (ml_dtypes.float8_e5m2, 14)}[fmt]
    v = np.moveaxis(np.asarray(x, np.float32).astype(ml_dtypes.bfloat16).astype(np.float64), axis, -1)
    blocks = v.reshape(v.shape[:-1] + (-1, 32))
    amax = np.abs(blocks).max(-1, keepdims=True)
    byte = np.maximum(np.where(amax > 0, np.frexp(amax)[1] - 1 + 127, 0) - down, 1)
    scale = np.exp2(byte - 127.0)
    codes = (blocks / scale).astype(np.float32).astype(dtype).astype(np.float64)
    return np.moveaxis((codes * scale).reshape(v.shape), -1, axis)


WIDE = False


def mx_kscale(k):
    if not WIDE:
        return np.ones(k)
    levels = np.array([10, -10, 5, -5, 0])
    if k % 512:
        return np.exp2(np.random.permutation(np.resize(levels, k // 32))).repeat(32)
    a = np.empty((k // 512, 16))
    for p in range(k // 512):
        a[p, :8] = np.random.permutation(np.resize(levels, 8))
        for g in range(8):
            far = levels[np.abs(levels - a[p, g]) >= 10]
            a[p, g + 8] = far[np.random.randint(len(far))]
    return np.exp2(a.ravel()).repeat(32)


def f64(x):
    return np.asarray(x).astype(np.float64)


def striped(idx):
    return np.tile(idx.reshape(-1, 16).T, (8, 1)).astype(np.uint16)


def unstriped(offs):
    return offs[:16].T.reshape(-1).astype(np.int64)


E2M1 = np.array([0.0, 0.5, 1.0, 1.5, 2.0, 3.0, 4.0, 6.0, -0.0, -0.5, -1.0, -1.5, -2.0, -3.0, -4.0, -6.0])


def pack_weight(w, fmt):
    k, n = w.shape
    w = f64(np.asarray(w, np.float32).astype(ml_dtypes.bfloat16)).reshape(k // 32, 32, n)
    amax = np.abs(w).max(1)
    if fmt == "e4m3":
        byte = np.frexp(amax)[1] - 1 + 127 - 7
    else:
        mant, ex = np.frexp(amax / 6.0)
        byte = np.where(mant > 0.5, ex, ex - 1) + 127
    byte = np.clip(np.where(amax > 0, byte, 1), 1, 254)
    scaled = (w * np.exp2(127.0 - byte)[:, None, :]).reshape(k, n).astype(np.float32)
    by_word = np.ascontiguousarray(scaled.reshape(k // 512, 128, 4, n).transpose(0, 1, 3, 2))
    if fmt == "e4m3":
        words = by_word.astype(ml_dtypes.float8_e4m3fn).view(np.uint8)
    else:
        c = by_word.astype(ml_dtypes.float4_e2m1fn).view(np.uint8) & 0xF
        words = (c[..., 0::2] | (c[..., 1::2] << 4)).reshape(k // 512, 128, 2 * n)
    return np.ascontiguousarray(words), np.ascontiguousarray(byte.astype(np.uint8).reshape(k // 512, 16, n))


def unpack_weight(words, scales, fmt):
    g, _, n = scales.shape
    words = np.ascontiguousarray(words).reshape(g, 128, n, -1)
    if fmt == "e4m3":
        vals = words.view(ml_dtypes.float8_e4m3fn).astype(np.float64)
    else:
        nib = np.empty((g, 128, n, 4), np.uint8)
        nib[..., 0::2] = words & 0xF
        nib[..., 1::2] = words >> 4
        vals = E2M1[nib]
    vals = vals * np.repeat(np.exp2(scales.astype(np.float64) - 127.0), 8, axis=1)[..., None]
    return vals.transpose(0, 1, 3, 2).reshape(g * 512, n)


def gelu(v):
    return 0.5 * v * (1.0 + np.tanh(np.sqrt(2.0 / np.pi) * (v + 0.044715 * v**3)))


K, K2, H, N, T, S = 1024, 512, 1024, 512, 4096, 1024

def setup_inputs():
    n = np.random.standard_normal
    s = mx_kscale(K)[:, None]
    s2 = mx_kscale(K2)[:, None]
    u = mx_kscale(H)[:, None]
    d = {}
    d["tab_words"], d["tab_scales"] = pack_weight(n((K, T)) * s, "e4m3")
    d["offs"] = striped(np.random.permutation(T)[:S])
    d["xs_words"], d["xs_scales"] = pack_weight(n((K2, S)) * s2, "e4m3")
    d["w1"] = (n((K, H)) / K**0.5 / s).astype(np.float32)
    d["w2_words"], d["w2_scales"] = pack_weight(n((K2, H)) / K2**0.5 / s2, "e2m1")
    d["gain"] = (u[:, 0] * np.exp(0.3 * n(H))).astype(np.float32)
    d["w3"] = (n((H, N)) / H**0.5 / u).astype(np.float32)
    d["w4_words"], d["w4_scales"] = pack_weight(n((H, N)) / H**0.5 / u, "e2m1")
    return d

def reference(tab_words, tab_scales, offs, xs_words, xs_scales, w1, w2_words, w2_scales, gain, w3, w4_words, w4_scales):
    v = unpack_weight(tab_words, tab_scales, "e4m3")[:, unstriped(offs)]
    xs = unpack_weight(xs_words, xs_scales, "e4m3")
    w2 = unpack_weight(w2_words, w2_scales, "e2m1")
    w4 = unpack_weight(w4_words, w4_scales, "e2m1")
    want = mxq(f64(w1), 0, "e4m3").T @ v
    have = w2.T @ xs
    diff = want - have
    act = 0.5 * diff * (1.0 + np.tanh(0.7978845608028654 * (diff + 0.044715 * diff**3)))
    h = act * f64(gain)[:, None]
    hq = mxq(h, 0, "e4m3")
    y1 = mxq(f64(w3), 0, "e4m3").T @ hq
    y2 = w4.T @ hq
    return np.maximum(y1, y2)

@@ -1,0 +1,236 @@
+from contextlib import ExitStack
+
+import concourse.mybir as mybir
+
+K, K2, H, N, T, S = 1024, 512, 1024, 512, 4096, 1024
+FLOPS = 2 * S * (K * H + K2 * H + 2 * H * N)
+
+F32 = mybir.dt.float32
+BF16 = mybir.dt.bfloat16
+I32 = mybir.dt.int32
+U32 = mybir.dt.uint32
+U16 = mybir.dt.uint16
+U8 = mybir.dt.uint8
+FP8X4 = mybir.dt.float8_e4m3fn_x4
+FP4X4 = mybir.dt.float4_e2m1fn_x4
+ACT = mybir.ActivationFunctionType
+ALU = mybir.AluOpType
+
+P = 128
+PACK = 4
+KP = P * PACK
+NT = 512
+
+
+def tile_list_plaza_stall_scores_kernel(tc, tab_words, tab_scales, offs, xs_words, xs_scales, w1,
+                                                  w2_words, w2_scales, gain, w3, w4_words, w4_scales, out):
+    nc = tc.nc
+    with ExitStack() as ctx:
+        keep = ctx.enter_context(tc.tile_pool(name="keep", bufs=1))
+        ring = ctx.enter_context(tc.tile_pool(name="ring", bufs=4))
+        outp = ctx.enter_context(tc.tile_pool(name="outp", bufs=8))
+        psum = ctx.enter_context(tc.psum_pool(name="psum", bufs=8))
+
+        def held(shape, dtype, name):
+            return keep.tile(shape, dtype, name=name, align_bytes=64)
+
+        offsets = keep.tile([P, S // 16], U16, name="offsets")
+        tab_w = [held([P, T], I32, f"tab_w{a}") for a in range(2)]
+        tab_s = held([P, T], U8, "tab_s")
+        xs_w = held([P, S], U32, "xs_w")
+        xs_s = held([P, S], U8, "xs_s")
+        w2_raw = held([P, 2 * H], U8, "w2_raw")
+        w2s_raw = held([P, H], U8, "w2s_raw")
+        w2_w = held([P, 2 * H], U8, "w2_w")
+        w2_s = held([P, H], U8, "w2_s")
+        w4_w = held([P, 2, 2 * N], U8, "w4_w")
+        w4_s = held([P, 2, N], U8, "w4_s")
+        gain_sb = held([P, 2, PACK], F32, "gain_sb")
+        w1_raw = {(a, b): held([P, PACK, KP], F32, f"w1_raw{a}{b}") for a in range(2) for b in range(2)}
+        w3_raw = [held([P, PACK, N], F32, f"w3_raw{a}") for a in range(2)]
+        warm = held([P, 1], F32, "warm")
+
+        nc.vector.memset(w2s_raw[:].bitcast(I32), 0)
+        nc.vector.memset(tab_s[:].bitcast(I32), 0)
+        nc.vector.memset(xs_s[:].bitcast(I32), 0)
+        nc.vector.memset(w4_s[:].rearrange("p a c -> p (a c)").bitcast(I32), 0)
+        nc.gpsimd.memset(warm[:], 0.0)
+        nc.scalar.activation(out=warm[:], in_=warm[:], func=ACT.Gelu_apprx_tanh)
+
+        def load_w1(a, b):
+            nc.sync.dma_start(out=w1_raw[a, b][:],
+                              in_=w1[a * KP:(a + 1) * KP, b * KP:(b + 1) * KP].rearrange("(p j) c -> p j c", j=PACK))
+
+        def load_tab(a, half):
+            cs = slice(half * T // 2, (half + 1) * T // 2)
+            nc.sync.dma_start(out=tab_w[a][:, cs], in_=tab_words[a].rearrange("p n t -> p (n t)").bitcast(I32)[:, cs])
+
+        nc.sync.dma_start(offsets[:], offs)
+        for q in range(4):
+            nc.sync.dma_start(out=w2s_raw[32 * q:32 * q + 4, :].bitcast(I32),
+                              in_=w2_scales[0, 4 * q:4 * q + 4, :].bitcast(I32))
+        nc.sync.dma_start(out=w2_raw[:].bitcast(I32), in_=w2_words[0].bitcast(I32))
+        nc.sync.dma_start(out=xs_w[:].bitcast(I32), in_=xs_words[0].rearrange("p n t -> p (n t)").bitcast(I32))
+        load_w1(0, 0)
+        load_tab(0, 0)
+        for q in range(4):
+            nc.sync.dma_start(out=tab_s[32 * q + 4:32 * q + 12, :].bitcast(I32),
+                              in_=tab_scales[:, 4 * q:4 * q + 4, :].bitcast(I32))
+        load_tab(0, 1)
+        for q in range(4):
+            nc.sync.dma_start(out=xs_s[32 * q:32 * q + 4, :].bitcast(I32),
+                              in_=xs_scales[0, 4 * q:4 * q + 4, :].bitcast(I32))
+        load_w1(1, 0)
+        load_tab(1, 0)
+        load_tab(1, 1)
+        nc.sync.dma_start(out=gain_sb[:], in_=gain.rearrange("(b p t) -> p b t", b=2, t=PACK))
+        load_w1(0, 1)
+        load_w1(1, 1)
+        nc.sync.dma_start(out=w4_w[:].bitcast(I32), in_=w4_words.rearrange("a p c -> p a c").bitcast(I32))
+        for q in range(4):
+            nc.sync.dma_start(out=w4_s[32 * q:32 * q + 4, :, :].bitcast(I32),
+                              in_=w4_scales[:, 4 * q:4 * q + 4, :].rearrange("a r c -> r a c").bitcast(I32))
+        for a in range(2):
+            nc.sync.dma_start(out=w3_raw[a][:], in_=w3[a * KP:(a + 1) * KP, :].rearrange("(p j) c -> p j c", j=PACK))
+
+        for b in range(2):
+            nc.vector.tensor_copy(
+                out=w2_w[:, 2 * KP * b:2 * KP * (b + 1)].rearrange("p (t m e) -> p m t e", t=PACK, e=2),
+                in_=w2_raw[:, 2 * KP * b:2 * KP * (b + 1)].rearrange("p (m t e) -> p m t e", t=PACK, e=2))
+        nc.vector.tensor_copy(out=w2_s[:].rearrange("p (b t m) -> p b t m", b=2, t=PACK),
+                              in_=w2s_raw[:].rearrange("p (b m t) -> p b t m", b=2, t=PACK))
+
+        w1_g, w1_c, w1_s = {}, {}, {}
+
+        def cast_w1(a, b, engines):
+            w1_g[a, b] = held([P, PACK * KP], BF16, f"w1_g{a}{b}")
+            dst = w1_g[a, b][:].rearrange("p (t m j) -> p m j t", t=PACK, j=PACK)
+            src = w1_raw[a, b][:].rearrange("p j (m t) -> p m j t", t=PACK)
+            for half, eng in enumerate(engines):
+                ms = slice(64 * half, 64 * (half + 1))
+                if eng == "s":
+                    nc.scalar.activation(out=dst[:, ms], in_=src[:, ms], func=ACT.Copy, scale=-1.0)
+                else:
+                    nc.vector.tensor_scalar(out=dst[:, ms], in0=src[:, ms], scalar1=-1.0, scalar2=None, op0=ALU.mult)
+
+        def quant_w1(a, b):
+            w1_c[a, b] = held([P, KP], U32, f"w1_c{a}{b}")
+            w1_s[a, b] = held([P, KP], U8, f"w1_s{a}{b}")
+            nc.vector.quantize_mx(out=w1_c[a, b][:].bitcast(FP8X4), scales=w1_s[a, b][:], in_=w1_g[a, b][:])
+
+        w3_g, w3_c, w3_s = {}, {}, {}
+
+        def cast_w3(a):
+            w3_g[a] = held([P, PACK * N], BF16, f"w3_g{a}")
+            dst = w3_g[a][:].rearrange("p (c i j) -> p c j i", i=4, j=PACK)
+            src = w3_raw[a][:].rearrange("p j (c i) -> p c j i", i=4)
+            for half in range(2):
+                cs = slice(64 * half, 64 * (half + 1))
+                nc.scalar.activation(out=dst[:, cs], in_=src[:, cs], func=ACT.Copy)
+
+        def quant_w3(a):
+            w3_c[a] = held([P, N], U32, f"w3_c{a}")
+            w3_s[a] = held([P, N], U8, f"w3_s{a}")
+            nc.vector.quantize_mx(out=w3_c[a][:].bitcast(FP8X4), scales=w3_s[a][:], in_=w3_g[a][:])
+
+        v_s = held([P, S], U8, "v_s")
+        v_w = {(a, jh): held([P, NT], U32, f"v_w{a}{jh}") for a in range(2) for jh in range(2)}
+
+        def gather_words(a, jh):
+            nc.vector.tensor_copy(out=v_w[a, jh][:],
+                                  in_=tab_w[a][:].bitcast(U32).indirect(offsets[:, 32 * jh:32 * (jh + 1)]))
+
+        cast_w1(0, 0, "ss")
+        quant_w1(0, 0)
+        nc.vector.tensor_copy(out=v_s[:], in_=tab_s[:].indirect(offsets[:]))
+        gather_words(0, 0)
+        gather_words(0, 1)
+        cast_w1(1, 0, "ss")
+        quant_w1(1, 0)
+        gather_words(1, 0)
+        gather_words(1, 1)
+
+        h_c, h_s, act, banks = {}, {}, {}, {}
+
+        def stage1(b, jh):
+            js = slice(NT * jh, NT * (jh + 1))
+            for t in range(PACK):
+                bank = psum.tile([P, NT], F32, name="bank", tag="bank")
+                banks[b, jh, t] = bank
+                c0 = KP * b + P * t
+                nc.tensor.matmul_mx(out=bank[:], lhsT=w2_w[:, 2 * c0:2 * (c0 + P)].bitcast(FP4X4),
+                                    lhsT_scale=w2_s[:, c0:c0 + P], rhs=xs_w[:, js].bitcast(FP8X4),
+                                    rhs_scale=xs_s[:, js], start=True, stop=False)
+                for a in range(2):
+                    nc.tensor.matmul_mx(out=bank[:], lhsT=w1_c[a, b][:, P * t:P * (t + 1)].bitcast(FP8X4),
+                                        lhsT_scale=w1_s[a, b][:, P * t:P * (t + 1)],
+                                        rhs=v_w[a, jh][:].bitcast(FP8X4), rhs_scale=v_s[4 + 4 * a:P, js],
+                                        start=False, stop=(a == 1))
+
+        def gelu(b, jh):
+            act[b, jh] = ring.tile([P, PACK, NT], F32, name="act", tag="act", align_bytes=64)
+            for t in range(PACK):
+                nc.scalar.activation(out=act[b, jh][:, t, :], in_=banks[b, jh, t][:], func=ACT.Gelu_apprx_tanh, scale=-1.0)
+
+        def make_h(b, jh):
+            h_bf = ring.tile([P, PACK * NT], BF16, name="h_bf", tag="h_bf", align_bytes=64)
+            dst = h_bf[:].rearrange("p (c i t) -> p c t i", i=4, t=PACK)
+            src = act[b, jh][:].rearrange("p t (c i) -> p c t i", i=4)
+            g = gain_sb[:, b, :].unsqueeze(1).unsqueeze(3).to_broadcast([P, 64, PACK, 4])
+            for half in range(2):
+                cs = slice(64 * half, 64 * (half + 1))
+                nc.vector.tensor_tensor(out=dst[:, cs], in0=src[:, cs], in1=g, op=ALU.mult)
+            h_c[b, jh] = held([P, NT], U32, f"h_c{b}{jh}")
+            h_s[b, jh] = held([P, NT], U8, f"h_s{b}{jh}")
+            for half in range(2):
+                cs = slice(256 * half, 256 * (half + 1))
+                nc.vector.quantize_mx(out=h_c[b, jh][:, cs].bitcast(FP8X4), scales=h_s[b, jh][:, cs],
+                                      in_=h_bf[:, 1024 * half:1024 * (half + 1)])
+
+        y2_sb = {}
+
+        def stage2_w4(jh, nt):
+            ns = slice(P * nt, P * (nt + 1))
+            y2 = psum.tile([P, NT], F32, name="y2", tag="bank")
+            for b in range(2):
+                nc.tensor.matmul_mx(out=y2[:], lhsT=w4_w[:, b, 2 * P * nt:2 * P * (nt + 1)].bitcast(FP4X4),
+                                    lhsT_scale=w4_s[:, b, ns], rhs=h_c[b, jh][:].bitcast(FP8X4),
+                                    rhs_scale=h_s[b, jh][:], start=(b == 0), stop=(b == 1))
+            y2_sb[jh, nt] = held([P, NT], F32, f"y2_sb{jh}{nt}")
+            nc.scalar.activation(out=y2_sb[jh, nt][:], in_=y2[:], func=ACT.Copy)
+
+        def stage2_w3(jh, nt):
+            ns = slice(P * nt, P * (nt + 1))
+            y1 = psum.tile([P, NT], F32, name="y1", tag="bank")
+            for b in range(2):
+                nc.tensor.matmul_mx(out=y1[:], lhsT=w3_c[b][:, ns].bitcast(FP8X4), lhsT_scale=w3_s[b][:, ns],
+                                    rhs=h_c[b, jh][:].bitcast(FP8X4), rhs_scale=h_s[b, jh][:],
+                                    start=(b == 0), stop=(b == 1))
+            res = outp.tile([P, NT], F32, name="res", tag="res")
+            nc.vector.tensor_tensor(out=res[:], in0=y1[:], in1=y2_sb[jh, nt][:], op=ALU.max)
+            nc.sync.dma_start(out=out[ns, NT * jh:NT * (jh + 1)], in_=res[:])
+
+        stage1(0, 0)
+        stage1(0, 1)
+        gelu(0, 0)
+        cast_w1(0, 1, "vv")
+        quant_w1(0, 1)
+        cast_w1(1, 1, "sv")
+        quant_w1(1, 1)
+        gelu(0, 1)
+        stage1(1, 0)
+        stage1(1, 1)
+        gelu(1, 0)
+        make_h(0, 0)
+        make_h(1, 0)
+        gelu(1, 1)
+        for a in range(2):
+            cast_w3(a)
+            quant_w3(a)
+        make_h(0, 1)
+        make_h(1, 1)
+        for jh in range(2):
+            for nt in range(N // P):
+                stage2_w4(jh, nt)
+            for nt in range(N // P):
+                stage2_w3(jh, nt)

@@ -1,6 +1,7 @@
 from contextlib import ExitStack
 
 import concourse.mybir as mybir
+from concourse.masks import make_identity
 
 K, K2, H, N, T, S = 1024, 512, 1024, 512, 4096, 1024
 FLOPS = 2 * S * (K * H + K2 * H + 2 * H * N)
@@ -29,7 +30,8 @@ def tile_list_plaza_stall_scores_kernel(tc, tab_words, tab_scales, offs, xs_word
         keep = ctx.enter_context(tc.tile_pool(name="keep", bufs=1))
         ring = ctx.enter_context(tc.tile_pool(name="ring", bufs=4))
         outp = ctx.enter_context(tc.tile_pool(name="outp", bufs=8))
-        psum = ctx.enter_context(tc.psum_pool(name="psum", bufs=8))
+        psum = ctx.enter_context(tc.psum_pool(name="psum", bufs=7))
+        gps = ctx.enter_context(tc.psum_pool(name="gps", bufs=1))
 
         def held(shape, dtype, name):
             return keep.tile(shape, dtype, name=name, align_bytes=64)
@@ -45,16 +47,21 @@ def tile_list_plaza_stall_scores_kernel(tc, tab_words, tab_scales, offs, xs_word
         w2_s = held([P, H], U8, "w2_s")
         w4_w = held([P, 2, 2 * N], U8, "w4_w")
         w4_s = held([P, 2, N], U8, "w4_s")
-        gain_sb = held([P, 2, PACK], F32, "gain_sb")
+        gain_sb = held([P, P], F32, "gain_sb")
+        gain_t = held([P, P], F32, "gain_t")
+        ident = held([P, P], F32, "ident")
+        gain_ps = gps.tile([P, 2 * P], F32, name="gain_ps")
         w1_raw = {(a, b): held([P, PACK, KP], F32, f"w1_raw{a}{b}") for a in range(2) for b in range(2)}
         w3_raw = [held([P, PACK, N], F32, f"w3_raw{a}") for a in range(2)]
         warm = held([P, 1], F32, "warm")
 
-        nc.vector.memset(w2s_raw[:].bitcast(I32), 0)
         nc.vector.memset(tab_s[:].bitcast(I32), 0)
+        nc.vector.memset(w2s_raw[:].bitcast(I32), 0)
         nc.vector.memset(xs_s[:].bitcast(I32), 0)
         nc.vector.memset(w4_s[:].rearrange("p a c -> p (a c)").bitcast(I32), 0)
+        nc.vector.memset(gain_sb[:], 0.0)
         nc.gpsimd.memset(warm[:], 0.0)
+        make_identity(nc, ident[:])
         nc.scalar.activation(out=warm[:], in_=warm[:], func=ACT.Gelu_apprx_tanh)
 
         def load_w1(a, b):
@@ -65,40 +72,45 @@ def tile_list_plaza_stall_scores_kernel(tc, tab_words, tab_scales, offs, xs_word
             cs = slice(half * T // 2, (half + 1) * T // 2)
             nc.sync.dma_start(out=tab_w[a][:, cs], in_=tab_words[a].rearrange("p n t -> p (n t)").bitcast(I32)[:, cs])
 
+        for q in range(4):
+            nc.gpsimd.dma_start(out=w4_s[32 * q:32 * q + 4, :, :].bitcast(I32),
+                                in_=w4_scales[:, 4 * q:4 * q + 4, :].rearrange("a r c -> r a c").bitcast(I32))
         nc.sync.dma_start(offsets[:], offs)
+        load_w1(0, 0)
+        for a in range(2):
+            for q in range(4):
+                nc.sync.dma_start(out=tab_s[32 * q + 4 + 4 * a:32 * q + 8 + 4 * a, :].bitcast(I32),
+                                  in_=tab_scales[a, 4 * q:4 * q + 4, :].bitcast(I32))
+        load_tab(0, 0)
+        load_tab(0, 1)
         for q in range(4):
             nc.sync.dma_start(out=w2s_raw[32 * q:32 * q + 4, :].bitcast(I32),
                               in_=w2_scales[0, 4 * q:4 * q + 4, :].bitcast(I32))
         nc.sync.dma_start(out=w2_raw[:].bitcast(I32), in_=w2_words[0].bitcast(I32))
-        nc.sync.dma_start(out=xs_w[:].bitcast(I32), in_=xs_words[0].rearrange("p n t -> p (n t)").bitcast(I32))
-        load_w1(0, 0)
-        load_tab(0, 0)
-        for q in range(4):
-            nc.sync.dma_start(out=tab_s[32 * q + 4:32 * q + 12, :].bitcast(I32),
-                              in_=tab_scales[:, 4 * q:4 * q + 4, :].bitcast(I32))
-        load_tab(0, 1)
+        nc.sync.dma_start(out=gain_sb[:, 0:2 * PACK].rearrange("p (b t) -> p b t", b=2),
+                          in_=gain.rearrange("(b p t) -> p b t", b=2, t=PACK))
+        load_w1(1, 0)
+        load_tab(1, 0)
         for q in range(4):
             nc.sync.dma_start(out=xs_s[32 * q:32 * q + 4, :].bitcast(I32),
                               in_=xs_scales[0, 4 * q:4 * q + 4, :].bitcast(I32))
-        load_w1(1, 0)
-        load_tab(1, 0)
+        nc.sync.dma_start(out=xs_w[:].bitcast(I32), in_=xs_words[0].rearrange("p n t -> p (n t)").bitcast(I32))
         load_tab(1, 1)
-        nc.sync.dma_start(out=gain_sb[:], in_=gain.rearrange("(b p t) -> p b t", b=2, t=PACK))
         load_w1(0, 1)
         load_w1(1, 1)
         nc.sync.dma_start(out=w4_w[:].bitcast(I32), in_=w4_words.rearrange("a p c -> p a c").bitcast(I32))
-        for q in range(4):
-            nc.sync.dma_start(out=w4_s[32 * q:32 * q + 4, :, :].bitcast(I32),
-                              in_=w4_scales[:, 4 * q:4 * q + 4, :].rearrange("a r c -> r a c").bitcast(I32))
         for a in range(2):
             nc.sync.dma_start(out=w3_raw[a][:], in_=w3[a * KP:(a + 1) * KP, :].rearrange("(p j) c -> p j c", j=PACK))
 
-        for b in range(2):
-            nc.vector.tensor_copy(
-                out=w2_w[:, 2 * KP * b:2 * KP * (b + 1)].rearrange("p (t m e) -> p m t e", t=PACK, e=2),
-                in_=w2_raw[:, 2 * KP * b:2 * KP * (b + 1)].rearrange("p (m t e) -> p m t e", t=PACK, e=2))
-        nc.vector.tensor_copy(out=w2_s[:].rearrange("p (b t m) -> p b t m", b=2, t=PACK),
-                              in_=w2s_raw[:].rearrange("p (b m t) -> p b t m", b=2, t=PACK))
+        nc.tensor.transpose(gain_ps[:, P:2 * P], gain_sb[:], ident[:])
+        nc.scalar.activation(out=gain_t[:], in_=gain_ps[:, P:2 * P], func=ACT.Copy)
+        nc.tensor.transpose(gain_ps[:, 0:P], gain_t[:], ident[:])
+
+        def deal_w2():
+            nc.vector.tensor_copy(out=w2_w[:].bitcast(U16).rearrange("p (b t m) -> p b t m", b=2, t=PACK),
+                                  in_=w2_raw[:].bitcast(U16).rearrange("p (b m t) -> p b t m", b=2, t=PACK))
+            nc.vector.tensor_copy(out=w2_s[:].rearrange("p (b t m) -> p b t m", b=2, t=PACK),
+                                  in_=w2s_raw[:].rearrange("p (b m t) -> p b t m", b=2, t=PACK))
 
         w1_g, w1_c, w1_s = {}, {}, {}
 
@@ -122,11 +134,11 @@ def tile_list_plaza_stall_scores_kernel(tc, tab_words, tab_scales, offs, xs_word
 
         def cast_w3(a):
             w3_g[a] = held([P, PACK * N], BF16, f"w3_g{a}")
-            dst = w3_g[a][:].rearrange("p (c i j) -> p c j i", i=4, j=PACK)
-            src = w3_raw[a][:].rearrange("p j (c i) -> p c j i", i=4)
-            for half in range(2):
-                cs = slice(64 * half, 64 * (half + 1))
-                nc.scalar.activation(out=dst[:, cs], in_=src[:, cs], func=ACT.Copy)
+            dst = w3_g[a][:].rearrange("p (c j) -> p c j", j=PACK)
+            src = w3_raw[a][:].rearrange("p j c -> p c j")
+            for part in range(4):
+                cs = slice(128 * part, 128 * (part + 1))
+                nc.gpsimd.tensor_scalar(out=dst[:, cs], in0=src[:, cs], scalar1=1.0, scalar2=0.0, op0=ALU.mult, op1=ALU.add)
 
         def quant_w3(a):
             w3_c[a] = held([P, N], U32, f"w3_c{a}")
@@ -145,6 +157,7 @@ def tile_list_plaza_stall_scores_kernel(tc, tab_words, tab_scales, offs, xs_word
         nc.vector.tensor_copy(out=v_s[:], in_=tab_s[:].indirect(offsets[:]))
         gather_words(0, 0)
         gather_words(0, 1)
+        deal_w2()
         cast_w1(1, 0, "ss")
         quant_w1(1, 0)
         gather_words(1, 0)
@@ -158,14 +171,17 @@ def tile_list_plaza_stall_scores_kernel(tc, tab_words, tab_scales, offs, xs_word
                 bank = psum.tile([P, NT], F32, name="bank", tag="bank")
                 banks[b, jh, t] = bank
                 c0 = KP * b + P * t
-                nc.tensor.matmul_mx(out=bank[:], lhsT=w2_w[:, 2 * c0:2 * (c0 + P)].bitcast(FP4X4),
-                                    lhsT_scale=w2_s[:, c0:c0 + P], rhs=xs_w[:, js].bitcast(FP8X4),
-                                    rhs_scale=xs_s[:, js], start=True, stop=False)
-                for a in range(2):
-                    nc.tensor.matmul_mx(out=bank[:], lhsT=w1_c[a, b][:, P * t:P * (t + 1)].bitcast(FP8X4),
-                                        lhsT_scale=w1_s[a, b][:, P * t:P * (t + 1)],
-                                        rhs=v_w[a, jh][:].bitcast(FP8X4), rhs_scale=v_s[4 + 4 * a:P, js],
-                                        start=False, stop=(a == 1))
+                for step in range(3):
+                    if step == 1:
+                        nc.tensor.matmul_mx(out=bank[:], lhsT=w2_w[:, 2 * c0:2 * (c0 + P)].bitcast(FP4X4),
+                                            lhsT_scale=w2_s[:, c0:c0 + P], rhs=xs_w[:, js].bitcast(FP8X4),
+                                            rhs_scale=xs_s[:, js], start=False, stop=False)
+                    else:
+                        a = step // 2
+                        nc.tensor.matmul_mx(out=bank[:], lhsT=w1_c[a, b][:, P * t:P * (t + 1)].bitcast(FP8X4),
+                                            lhsT_scale=w1_s[a, b][:, P * t:P * (t + 1)],
+                                            rhs=v_w[a, jh][:].bitcast(FP8X4), rhs_scale=v_s[4 + 4 * a:P, js],
+                                            start=(a == 0), stop=(a == 1))
 
         def gelu(b, jh):
             act[b, jh] = ring.tile([P, PACK, NT], F32, name="act", tag="act", align_bytes=64)
@@ -174,11 +190,11 @@ def tile_list_plaza_stall_scores_kernel(tc, tab_words, tab_scales, offs, xs_word
 
         def make_h(b, jh):
             h_bf = ring.tile([P, PACK * NT], BF16, name="h_bf", tag="h_bf", align_bytes=64)
-            dst = h_bf[:].rearrange("p (c i t) -> p c t i", i=4, t=PACK)
-            src = act[b, jh][:].rearrange("p t (c i) -> p c t i", i=4)
-            g = gain_sb[:, b, :].unsqueeze(1).unsqueeze(3).to_broadcast([P, 64, PACK, 4])
+            dst = h_bf[:].rearrange("p (c i t) -> p c t i", i=2, t=PACK)
+            src = act[b, jh][:].rearrange("p t (c i) -> p c t i", i=2)
+            g = gain_ps[:, PACK * b:PACK * (b + 1)].unsqueeze(1).unsqueeze(3).to_broadcast([P, 128, PACK, 2])
             for half in range(2):
-                cs = slice(64 * half, 64 * (half + 1))
+                cs = slice(128 * half, 128 * (half + 1))
                 nc.vector.tensor_tensor(out=dst[:, cs], in0=src[:, cs], in1=g, op=ALU.mult)
             h_c[b, jh] = held([P, NT], U32, f"h_c{b}{jh}")
             h_s[b, jh] = held([P, NT], U8, f"h_s{b}{jh}")
@@ -207,27 +223,31 @@ def tile_list_plaza_stall_scores_kernel(tc, tab_words, tab_scales, offs, xs_word
                                     rhs=h_c[b, jh][:].bitcast(FP8X4), rhs_scale=h_s[b, jh][:],
                                     start=(b == 0), stop=(b == 1))
             res = outp.tile([P, NT], F32, name="res", tag="res")
-            nc.vector.tensor_tensor(out=res[:], in0=y1[:], in1=y2_sb[jh, nt][:], op=ALU.max)
-            nc.sync.dma_start(out=out[ns, NT * jh:NT * (jh + 1)], in_=res[:])
+            parts = 2 if (jh, nt) == (1, 3) else 1
+            w = NT // parts
+            for i in range(parts):
+                cs = slice(w * i, w * (i + 1))
+                nc.vector.tensor_tensor(out=res[:, cs], in0=y1[:, cs], in1=y2_sb[jh, nt][:, cs], op=ALU.max)
+                nc.sync.dma_start(out=out[ns, NT * jh + w * i:NT * jh + w * (i + 1)], in_=res[:, cs])
 
         stage1(0, 0)
         stage1(0, 1)
         gelu(0, 0)
         cast_w1(0, 1, "vv")
         quant_w1(0, 1)
-        cast_w1(1, 1, "sv")
+        cast_w1(1, 1, "ss")
         quant_w1(1, 1)
         gelu(0, 1)
         stage1(1, 0)
         stage1(1, 1)
         gelu(1, 0)
         make_h(0, 0)
+        make_h(0, 1)
         make_h(1, 0)
         gelu(1, 1)
         for a in range(2):
             cast_w3(a)
             quant_w3(a)
-        make_h(0, 1)
         make_h(1, 1)
         for jh in range(2):
             for nt in range(N // P):

from contextlib import ExitStack

import concourse.mybir as mybir
from concourse.masks import make_identity

K, K2, H, N, T, S = 1024, 512, 1024, 512, 4096, 1024
FLOPS = 2 * S * (K * H + K2 * H + 2 * H * N)

F32 = mybir.dt.float32
BF16 = mybir.dt.bfloat16
I32 = mybir.dt.int32
U32 = mybir.dt.uint32
U16 = mybir.dt.uint16
U8 = mybir.dt.uint8
FP8X4 = mybir.dt.float8_e4m3fn_x4
FP4X4 = mybir.dt.float4_e2m1fn_x4
ACT = mybir.ActivationFunctionType
ALU = mybir.AluOpType

P = 128
PACK = 4
KP = P * PACK
NT = 512


def tile_list_plaza_stall_scores_kernel(tc, tab_words, tab_scales, offs, xs_words, xs_scales, w1,
                                                  w2_words, w2_scales, gain, w3, w4_words, w4_scales, out):
    nc = tc.nc
    with ExitStack() as ctx:
        keep = ctx.enter_context(tc.tile_pool(name="keep", bufs=1))
        ring = ctx.enter_context(tc.tile_pool(name="ring", bufs=4))
        outp = ctx.enter_context(tc.tile_pool(name="outp", bufs=8))
        psum = ctx.enter_context(tc.psum_pool(name="psum", bufs=7))
        gps = ctx.enter_context(tc.psum_pool(name="gps", bufs=1))

        def held(shape, dtype, name):
            return keep.tile(shape, dtype, name=name, align_bytes=64)

        offsets = keep.tile([P, S // 16], U16, name="offsets")
        tab_w = [held([P, T], I32, f"tab_w{a}") for a in range(2)]
        tab_s = held([P, T], U8, "tab_s")
        xs_w = held([P, S], U32, "xs_w")
        xs_s = held([P, S], U8, "xs_s")
        w2_raw = held([P, 2 * H], U8, "w2_raw")
        w2s_raw = held([P, H], U8, "w2s_raw")
        w2_w = held([P, 2 * H], U8, "w2_w")
        w2_s = held([P, H], U8, "w2_s")
        w4_w = held([P, 2, 2 * N], U8, "w4_w")
        w4_s = held([P, 2, N], U8, "w4_s")
        gain_sb = held([P, P], F32, "gain_sb")
        gain_t = held([P, P], F32, "gain_t")
        ident = held([P, P], F32, "ident")
        gain_ps = gps.tile([P, 2 * P], F32, name="gain_ps")
        w1_raw = {(a, b): held([P, PACK, KP], F32, f"w1_raw{a}{b}") for a in range(2) for b in range(2)}
        w3_raw = [held([P, PACK, N], F32, f"w3_raw{a}") for a in range(2)]
        warm = held([P, 1], F32, "warm")

        nc.vector.memset(tab_s[:].bitcast(I32), 0)
        nc.vector.memset(w2s_raw[:].bitcast(I32), 0)
        nc.vector.memset(xs_s[:].bitcast(I32), 0)
        nc.vector.memset(w4_s[:].rearrange("p a c -> p (a c)").bitcast(I32), 0)
        nc.vector.memset(gain_sb[:], 0.0)
        nc.gpsimd.memset(warm[:], 0.0)
        make_identity(nc, ident[:])
        nc.scalar.activation(out=warm[:], in_=warm[:], func=ACT.Gelu_apprx_tanh)

        def load_w1(a, b):
            nc.sync.dma_start(out=w1_raw[a, b][:],
                              in_=w1[a * KP:(a + 1) * KP, b * KP:(b + 1) * KP].rearrange("(p j) c -> p j c", j=PACK))

        def load_tab(a, half):
            cs = slice(half * T // 2, (half + 1) * T // 2)
            nc.sync.dma_start(out=tab_w[a][:, cs], in_=tab_words[a].rearrange("p n t -> p (n t)").bitcast(I32)[:, cs])

        for q in range(4):
            nc.gpsimd.dma_start(out=w4_s[32 * q:32 * q + 4, :, :].bitcast(I32),
                                in_=w4_scales[:, 4 * q:4 * q + 4, :].rearrange("a r c -> r a c").bitcast(I32))
        nc.sync.dma_start(offsets[:], offs)
        load_w1(0, 0)
        for a in range(2):
            for q in range(4):
                nc.sync.dma_start(out=tab_s[32 * q + 4 + 4 * a:32 * q + 8 + 4 * a, :].bitcast(I32),
                                  in_=tab_scales[a, 4 * q:4 * q + 4, :].bitcast(I32))
        load_tab(0, 0)
        load_tab(0, 1)
        for q in range(4):
            nc.sync.dma_start(out=w2s_raw[32 * q:32 * q + 4, :].bitcast(I32),
                              in_=w2_scales[0, 4 * q:4 * q + 4, :].bitcast(I32))
        nc.sync.dma_start(out=w2_raw[:].bitcast(I32), in_=w2_words[0].bitcast(I32))
        nc.sync.dma_start(out=gain_sb[:, 0:2 * PACK].rearrange("p (b t) -> p b t", b=2),
                          in_=gain.rearrange("(b p t) -> p b t", b=2, t=PACK))
        load_w1(1, 0)
        load_tab(1, 0)
        for q in range(4):
            nc.sync.dma_start(out=xs_s[32 * q:32 * q + 4, :].bitcast(I32),
                              in_=xs_scales[0, 4 * q:4 * q + 4, :].bitcast(I32))
        nc.sync.dma_start(out=xs_w[:].bitcast(I32), in_=xs_words[0].rearrange("p n t -> p (n t)").bitcast(I32))
        load_tab(1, 1)
        load_w1(0, 1)
        load_w1(1, 1)
        nc.sync.dma_start(out=w4_w[:].bitcast(I32), in_=w4_words.rearrange("a p c -> p a c").bitcast(I32))
        for a in range(2):
            nc.sync.dma_start(out=w3_raw[a][:], in_=w3[a * KP:(a + 1) * KP, :].rearrange("(p j) c -> p j c", j=PACK))

        nc.tensor.transpose(gain_ps[:, P:2 * P], gain_sb[:], ident[:])
        nc.scalar.activation(out=gain_t[:], in_=gain_ps[:, P:2 * P], func=ACT.Copy)
        nc.tensor.transpose(gain_ps[:, 0:P], gain_t[:], ident[:])

        def deal_w2():
            nc.vector.tensor_copy(out=w2_w[:].bitcast(U16).rearrange("p (b t m) -> p b t m", b=2, t=PACK),
                                  in_=w2_raw[:].bitcast(U16).rearrange("p (b m t) -> p b t m", b=2, t=PACK))
            nc.vector.tensor_copy(out=w2_s[:].rearrange("p (b t m) -> p b t m", b=2, t=PACK),
                                  in_=w2s_raw[:].rearrange("p (b m t) -> p b t m", b=2, t=PACK))

        w1_g, w1_c, w1_s = {}, {}, {}

        def cast_w1(a, b, engines):
            w1_g[a, b] = held([P, PACK * KP], BF16, f"w1_g{a}{b}")
            dst = w1_g[a, b][:].rearrange("p (t m j) -> p m j t", t=PACK, j=PACK)
            src = w1_raw[a, b][:].rearrange("p j (m t) -> p m j t", t=PACK)
            for half, eng in enumerate(engines):
                ms = slice(64 * half, 64 * (half + 1))
                if eng == "s":
                    nc.scalar.activation(out=dst[:, ms], in_=src[:, ms], func=ACT.Copy, scale=-1.0)
                else:
                    nc.vector.tensor_scalar(out=dst[:, ms], in0=src[:, ms], scalar1=-1.0, scalar2=None, op0=ALU.mult)

        def quant_w1(a, b):
            w1_c[a, b] = held([P, KP], U32, f"w1_c{a}{b}")
            w1_s[a, b] = held([P, KP], U8, f"w1_s{a}{b}")
            nc.vector.quantize_mx(out=w1_c[a, b][:].bitcast(FP8X4), scales=w1_s[a, b][:], in_=w1_g[a, b][:])

        w3_g, w3_c, w3_s = {}, {}, {}

        def cast_w3(a):
            w3_g[a] = held([P, PACK * N], BF16, f"w3_g{a}")
            dst = w3_g[a][:].rearrange("p (c j) -> p c j", j=PACK)
            src = w3_raw[a][:].rearrange("p j c -> p c j")
            for part in range(4):
                cs = slice(128 * part, 128 * (part + 1))
                nc.gpsimd.tensor_scalar(out=dst[:, cs], in0=src[:, cs], scalar1=1.0, scalar2=0.0, op0=ALU.mult, op1=ALU.add)

        def quant_w3(a):
            w3_c[a] = held([P, N], U32, f"w3_c{a}")
            w3_s[a] = held([P, N], U8, f"w3_s{a}")
            nc.vector.quantize_mx(out=w3_c[a][:].bitcast(FP8X4), scales=w3_s[a][:], in_=w3_g[a][:])

        v_s = held([P, S], U8, "v_s")
        v_w = {(a, jh): held([P, NT], U32, f"v_w{a}{jh}") for a in range(2) for jh in range(2)}

        def gather_words(a, jh):
            nc.vector.tensor_copy(out=v_w[a, jh][:],
                                  in_=tab_w[a][:].bitcast(U32).indirect(offsets[:, 32 * jh:32 * (jh + 1)]))

        cast_w1(0, 0, "ss")
        quant_w1(0, 0)
        nc.vector.tensor_copy(out=v_s[:], in_=tab_s[:].indirect(offsets[:]))
        gather_words(0, 0)
        gather_words(0, 1)
        deal_w2()
        cast_w1(1, 0, "ss")
        quant_w1(1, 0)
        gather_words(1, 0)
        gather_words(1, 1)

        h_c, h_s, act, banks = {}, {}, {}, {}

        def stage1(b, jh):
            js = slice(NT * jh, NT * (jh + 1))
            for t in range(PACK):
                bank = psum.tile([P, NT], F32, name="bank", tag="bank")
                banks[b, jh, t] = bank
                c0 = KP * b + P * t
                for step in range(3):
                    if step == 1:
                        nc.tensor.matmul_mx(out=bank[:], lhsT=w2_w[:, 2 * c0:2 * (c0 + P)].bitcast(FP4X4),
                                            lhsT_scale=w2_s[:, c0:c0 + P], rhs=xs_w[:, js].bitcast(FP8X4),
                                            rhs_scale=xs_s[:, js], start=False, stop=False)
                    else:
                        a = step // 2
                        nc.tensor.matmul_mx(out=bank[:], lhsT=w1_c[a, b][:, P * t:P * (t + 1)].bitcast(FP8X4),
                                            lhsT_scale=w1_s[a, b][:, P * t:P * (t + 1)],
                                            rhs=v_w[a, jh][:].bitcast(FP8X4), rhs_scale=v_s[4 + 4 * a:P, js],
                                            start=(a == 0), stop=(a == 1))

        def gelu(b, jh):
            act[b, jh] = ring.tile([P, PACK, NT], F32, name="act", tag="act", align_bytes=64)
            for t in range(PACK):
                nc.scalar.activation(out=act[b, jh][:, t, :], in_=banks[b, jh, t][:], func=ACT.Gelu_apprx_tanh, scale=-1.0)

        def make_h(b, jh):
            h_bf = ring.tile([P, PACK * NT], BF16, name="h_bf", tag="h_bf", align_bytes=64)
            dst = h_bf[:].rearrange("p (c i t) -> p c t i", i=2, t=PACK)
            src = act[b, jh][:].rearrange("p t (c i) -> p c t i", i=2)
            g = gain_ps[:, PACK * b:PACK * (b + 1)].unsqueeze(1).unsqueeze(3).to_broadcast([P, 128, PACK, 2])
            for half in range(2):
                cs = slice(128 * half, 128 * (half + 1))
                nc.vector.tensor_tensor(out=dst[:, cs], in0=src[:, cs], in1=g, op=ALU.mult)
            h_c[b, jh] = held([P, NT], U32, f"h_c{b}{jh}")
            h_s[b, jh] = held([P, NT], U8, f"h_s{b}{jh}")
            for half in range(2):
                cs = slice(256 * half, 256 * (half + 1))
                nc.vector.quantize_mx(out=h_c[b, jh][:, cs].bitcast(FP8X4), scales=h_s[b, jh][:, cs],
                                      in_=h_bf[:, 1024 * half:1024 * (half + 1)])

        y2_sb = {}

        def stage2_w4(jh, nt):
            ns = slice(P * nt, P * (nt + 1))
            y2 = psum.tile([P, NT], F32, name="y2", tag="bank")
            for b in range(2):
                nc.tensor.matmul_mx(out=y2[:], lhsT=w4_w[:, b, 2 * P * nt:2 * P * (nt + 1)].bitcast(FP4X4),
                                    lhsT_scale=w4_s[:, b, ns], rhs=h_c[b, jh][:].bitcast(FP8X4),
                                    rhs_scale=h_s[b, jh][:], start=(b == 0), stop=(b == 1))
            y2_sb[jh, nt] = held([P, NT], F32, f"y2_sb{jh}{nt}")
            nc.scalar.activation(out=y2_sb[jh, nt][:], in_=y2[:], func=ACT.Copy)

        def stage2_w3(jh, nt):
            ns = slice(P * nt, P * (nt + 1))
            y1 = psum.tile([P, NT], F32, name="y1", tag="bank")
            for b in range(2):
                nc.tensor.matmul_mx(out=y1[:], lhsT=w3_c[b][:, ns].bitcast(FP8X4), lhsT_scale=w3_s[b][:, ns],
                                    rhs=h_c[b, jh][:].bitcast(FP8X4), rhs_scale=h_s[b, jh][:],
                                    start=(b == 0), stop=(b == 1))
            res = outp.tile([P, NT], F32, name="res", tag="res")
            parts = 2 if (jh, nt) == (1, 3) else 1
            w = NT // parts
            for i in range(parts):
                cs = slice(w * i, w * (i + 1))
                nc.vector.tensor_tensor(out=res[:, cs], in0=y1[:, cs], in1=y2_sb[jh, nt][:, cs], op=ALU.max)
                nc.sync.dma_start(out=out[ns, NT * jh + w * i:NT * jh + w * (i + 1)], in_=res[:, cs])

        stage1(0, 0)
        stage1(0, 1)
        gelu(0, 0)
        cast_w1(0, 1, "vv")
        quant_w1(0, 1)
        cast_w1(1, 1, "ss")
        quant_w1(1, 1)
        gelu(0, 1)
        stage1(1, 0)
        stage1(1, 1)
        gelu(1, 0)
        make_h(0, 0)
        make_h(0, 1)
        make_h(1, 0)
        gelu(1, 1)
        for a in range(2):
            cast_w3(a)
            quant_w3(a)
        make_h(1, 1)
        for jh in range(2):
            for nt in range(N // P):
                stage2_w4(jh, nt)
            for nt in range(N // P):
                stage2_w3(jh, nt)
